import numpy as np
import ml_dtypes


def mxq(x, axis, fmt="e4m3"):
    dtype, down = {"e4m3": (ml_dtypes.float8_e4m3fn, 7), "e5m2": (ml_dtypes.float8_e5m2, 14)}[fmt]
    v = np.moveaxis(np.asarray(x, np.float32).astype(ml_dtypes.bfloat16).astype(np.float64), axis, -1)
    blocks = v.reshape(v.shape[:-1] + (-1, 32))
    amax = np.abs(blocks).max(-1, keepdims=True)
    byte = np.maximum(np.where(amax > 0, np.frexp(amax)[1] - 1 + 127, 0) - down, 1)
    scale = np.exp2(byte - 127.0)
    codes = (blocks / scale).astype(np.float32).astype(dtype).astype(np.float64)
    return np.moveaxis((codes * scale).reshape(v.shape), -1, axis)


WIDE = False


def mx_kscale(k):
    if not WIDE:
        return np.ones(k)
    levels = np.array([10, -10, 5, -5, 0])
    if k % 512:
        return np.exp2(np.random.permutation(np.resize(levels, k // 32))).repeat(32)
    a = np.empty((k // 512, 16))
    for p in range(k // 512):
        a[p, :8] = np.random.permutation(np.resize(levels, 8))
        for g in range(8):
            far = levels[np.abs(levels - a[p, g]) >= 10]
            a[p, g + 8] = far[np.random.randint(len(far))]
    return np.exp2(a.ravel()).repeat(32)


BF16 = ml_dtypes.bfloat16


def bf(x):
    return np.asarray(x, np.float32).astype(BF16)


def f64(x):
    return np.asarray(x).astype(np.float64)


E2M1 = np.array([0.0, 0.5, 1.0, 1.5, 2.0, 3.0, 4.0, 6.0, -0.0, -0.5, -1.0, -1.5, -2.0, -3.0, -4.0, -6.0])


def pack_weight(w, fmt):
    k, n = w.shape
    w = f64(bf(w)).reshape(k // 32, 32, n)
    amax = np.abs(w).max(1)
    if fmt == "e4m3":
        byte = np.frexp(amax)[1] - 1 + 127 - 7
    else:
        mant, ex = np.frexp(amax / 6.0)
        byte = np.where(mant > 0.5, ex, ex - 1) + 127
    byte = np.clip(np.where(amax > 0, byte, 1), 1, 254)
    scaled = (w * np.exp2(127.0 - byte)[:, None, :]).reshape(k, n).astype(np.float32)
    by_word = np.ascontiguousarray(scaled.reshape(k // 512, 128, 4, n).transpose(0, 1, 3, 2))
    if fmt == "e4m3":
        words = by_word.astype(ml_dtypes.float8_e4m3fn).view(np.uint8)
    else:
        c = by_word.astype(ml_dtypes.float4_e2m1fn).view(np.uint8) & 0xF
        words = c[..., 0::2] | (c[..., 1::2] << 4)
    return np.ascontiguousarray(words), np.ascontiguousarray(byte.astype(np.uint8).reshape(k // 512, 16, n))


def unpack_weight(words, scales, fmt):
    g, p, n, _ = words.shape
    if fmt == "e4m3":
        vals = np.ascontiguousarray(words).view(ml_dtypes.float8_e4m3fn).astype(np.float64)
    else:
        nib = np.empty((g, p, n, 4), np.uint8)
        nib[..., 0::2] = words & 0xF
        nib[..., 1::2] = words >> 4
        vals = E2M1[nib]
    vals = vals * np.repeat(np.exp2(scales.astype(np.float64) - 127.0), 8, axis=1)[..., None]
    return vals.transpose(0, 1, 3, 2).reshape(g * 512, n)
def pack4(w):
    words, scales = pack_weight(w, "e2m1")
    return words.reshape(words.shape[0], 128, -1), scales


def unpack4(words, scales):
    return unpack_weight(words.reshape(words.shape[0], 128, -1, 2), scales, "e2m1")


M, C1, C2, N, R = 1024, 1024, 2048, 1024, 512


def draw0():
    s1, s2, t = mx_kscale(C1), mx_kscale(C2), mx_kscale(N)
    pinv_new = np.random.standard_normal((M, C1)) / np.sqrt(C1 + C2)
    pinv_old = np.random.standard_normal((M, C2)) / np.sqrt(C1 + C2)
    y_new = np.random.standard_normal((C1, N))
    y_old = np.random.standard_normal((C2, N))
    prog = np.random.standard_normal((N, R)) / np.sqrt(N)
    old_words, old_scales = pack4(y_old / s2[:, None])
    prog_words, prog_scales = pack4(prog / t[:, None])
    return {"pinv_new": bf(pinv_new * s1),
            "pinv_old": bf(pinv_old * s2),
            "y_new": bf(y_new / s1[:, None]),
            "old_words": old_words,
            "old_scales": old_scales,
            "control": bf(0.4 * np.random.standard_normal(N)),
            "inv_sd": bf((1 + 0.1 * np.random.standard_normal(N)) * t),
            "prog_words": prog_words,
            "prog_scales": prog_scales,
            "precision": bf(1 + 0.1 * np.random.standard_normal(M))}


def core(pinv_new, pinv_old, y_new, old_words, old_scales, control, inv_sd, prog_words, prog_scales, precision):
    new = mxq(f64(pinv_new), 1, "e4m3") @ mxq(f64(y_new), 0, "e4m3")
    old = mxq(f64(pinv_old), 1, "e4m3") @ unpack4(old_words, old_scales)
    effect = (new + old - f64(control)) * f64(inv_sd)
    score = mxq(effect, 1, "e4m3") @ unpack4(prog_words, prog_scales)
    return score * f64(precision)[:, None]


def e4m3fn_bytes(y):
    return np.clip(np.asarray(y, np.float64), -448.0, 448.0).astype(np.float32).astype(ml_dtypes.float8_e4m3fn).view(np.uint8)


def e4m3fn_values(b):
    return np.asarray(b, np.uint8).view(ml_dtypes.float8_e4m3fn).astype(np.float64)


def setup_inputs():
    d = draw0()
    x0 = np.asarray(d['pinv_old']).astype(np.float64)
    s = (np.max(np.abs(x0), axis=(0,), keepdims=True) / 448.0).astype(np.float32)
    out = {}
    for k, v in d.items():
        if k == 'pinv_old':
            out['pinv_old_bytes'] = e4m3fn_bytes(x0 / s.astype(np.float64))
            out['pinv_old_scale'] = s
        else:
            out[k] = v
    return out


def reference(pinv_new, pinv_old_bytes, pinv_old_scale, y_new, old_words, old_scales, control, inv_sd, prog_words, prog_scales, precision):
    return core(pinv_new, e4m3fn_values(pinv_old_bytes) * pinv_old_scale.astype(np.float64), y_new, old_words, old_scales, control, inv_sd, prog_words, prog_scales, precision)

@@ -1,0 +1,363 @@
+from contextlib import ExitStack
+
+import concourse.mybir as mybir
+from concourse.masks import make_identity
+
+M, C1, C2, N, R = 1024, 1024, 2048, 1024, 512
+FLOPS = 2 * M * N * (C1 + C2) + 2 * M * N * R
+
+F32 = mybir.dt.float32
+BF16 = mybir.dt.bfloat16
+U32 = mybir.dt.uint32
+I32 = mybir.dt.int32
+U8 = mybir.dt.uint8
+FP8 = mybir.dt.float8_e4m3fn
+E4M3X4 = mybir.dt.float8_e4m3fn_x4
+E2M1X4 = mybir.dt.float4_e2m1fn_x4
+MULT = mybir.AluOpType.mult
+ADD = mybir.AluOpType.add
+ACT = mybir.ActivationFunctionType
+
+
+def tile_perturb_seq_programmes_s3_kernel(
+    tc, pinv_new, pinv_old_bytes, pinv_old_scale, y_new, old_words, old_scales,
+    control, inv_sd, prog_words, prog_scales, precision, out,
+):
+    nc = tc.nc
+    with ExitStack() as ctx:
+        sb = ctx.enter_context(tc.tile_pool(name="sb", bufs=1))
+        psum = ctx.enter_context(tc.psum_pool(name="psum", bufs=1))
+        ctx.enter_context(tc.manual_schedule())
+
+        def tile(shape, dtype, name, tag=None):
+            return sb.tile(shape, dtype, name=name, tag=tag or name, align_bytes=64)
+
+        def bank(j, name):
+            return psum.tile([128, 512], F32, name=name, tag="bank%d" % j)
+
+        ident = tile([128, 128], F32, "ident")
+        w_raw = [tile([128, 4, 1024], U8, "w_raw%d" % q) for q in range(2)]
+        w = [tile([128, 4, 1024], U8, "w%d" % q) for q in range(2)]
+        s_raw = [tile([128, 4, 512], U8, "s_raw%d" % q) for q in range(2)]
+        s = [tile([128, 4, 512], U8, "s%d" % q) for q in range(2)]
+        pw = tile([128, 2, 1024], U8, "pw")
+        ps = tile([128, 2, 512], U8, "ps")
+        sc = [tile([128, 512], F32, "sc%d" % g) for g in range(4)]
+        x = [[tile([128, 4, 512], U8, "x%d%d" % (h, g)) for g in range(4)] for h in range(2)]
+        pn = [[tile([128, 2, 1024], BF16, "pn%d%d" % (h, i)) for i in range(2)] for h in range(2)]
+        y_raw = [[tile([128, 4, 512], BF16, "y_raw%d%d" % (q, g)) for g in range(2)] for q in range(2)]
+        yc = [[tile([128, 512], U32, "yc%d%d" % (q, g)) for g in range(2)] for q in range(2)]
+        ys = [[tile([128, 512], U8, "ys%d%d" % (q, g)) for g in range(2)] for q in range(2)]
+        vec = [tile([128, 8], BF16, "vec%d" % i) for i in range(3)]
+        vecf = tile([128, 3, 8], F32, "vecf")
+        nb0 = tile([128, 8], F32, "nb0")
+        nb = tile([128, 8], F32, "nb")
+        dummy = tile([128, 1], F32, "dummy")
+
+        nc.gpsimd.memset(s_raw[0][:].rearrange("p g n -> p (g n)").bitcast(I32), 0)
+        nc.gpsimd.memset(s_raw[1][:].rearrange("p g n -> p (g n)").bitcast(I32), 0)
+        nc.gpsimd.memset(ps[:].rearrange("p g n -> p (g n)").bitcast(I32), 0)
+        make_identity(nc, ident[:])
+        nc.gpsimd.dma_start(out=vec[0][:].rearrange("p (g t) -> p g t", t=4), in_=control.rearrange("(g p t) -> p g t", p=128, t=4))
+        nc.gpsimd.dma_start(out=vec[1][:].rearrange("p (g t) -> p g t", t=4), in_=inv_sd.rearrange("(g p t) -> p g t", p=128, t=4))
+        nc.gpsimd.dma_start(out=vec[2][:], in_=precision.rearrange("(p a) -> p a", a=8))
+        for i in range(3):
+            nc.gpsimd.tensor_copy(out=vecf[:, i, :], in_=vec[i][:])
+        nc.gpsimd.tensor_tensor(out=nb0[:], in0=vecf[:, 0, :], in1=vecf[:, 1, :], op=MULT)
+        nc.gpsimd.tensor_scalar(out=nb[:], in0=nb0[:], scalar1=-1.0, scalar2=0.0, op0=MULT, op1=ADD)
+        nc.vector.memset(dummy[:], 0.0)
+        nc.scalar.activation(out=dummy[:], in_=dummy[:], func=ACT.Identity)
+
+        xr = pinv_old_bytes.rearrange("(p a) k -> p a k", a=8)
+        pr = pinv_new.rearrange("(p a) k -> p a k", a=8)
+        sr = old_scales.rearrange("g r n -> r g n")
+        psr = prog_scales.rearrange("g r n -> r g n")
+
+        def load_words(q):
+            c = slice(1024 * q, 1024 * q + 1024)
+            nc.sync.dma_start(out=w_raw[q][:], in_=old_words[:, :, c].rearrange("g p b -> p g b"))
+
+        def load_y(q, g):
+            nc.sync.dma_start(out=y_raw[q][g][:], in_=y_new[512 * g : 512 * g + 512, 512 * q : 512 * q + 512].rearrange("(p j) n -> p j n", j=4))
+
+        def load_sc(g):
+            nc.sync.dma_start(out=sc[g][:], in_=pinv_old_scale[:, 512 * g : 512 * g + 512].rearrange("o k -> (o k)").partition_broadcast(128))
+
+        def load_x(h, g):
+            nc.sync.dma_start(out=x[h][g][:], in_=xr[:, 4 * h : 4 * h + 4, 512 * g : 512 * g + 512])
+
+        def load_pn(h, i):
+            nc.sync.dma_start(out=pn[h][i][:], in_=pr[:, 4 * h + 2 * i : 4 * h + 2 * i + 2, :])
+
+        def load_scales(q):
+            for b in range(4):
+                nc.sync.dma_start(out=s_raw[q][32 * b : 32 * b + 4, :, :].bitcast(I32), in_=sr[4 * b : 4 * b + 4, :, 512 * q : 512 * q + 512].bitcast(I32))
+
+        load_words(0)
+        load_sc(0)
+        load_x(0, 0)
+        load_scales(0)
+        load_pn(0, 0)
+        load_pn(0, 1)
+        load_sc(1)
+        load_x(0, 1)
+        load_y(0, 0)
+        load_sc(2)
+        load_x(0, 2)
+        load_y(0, 1)
+        load_sc(3)
+        load_x(0, 3)
+        load_pn(1, 0)
+        load_pn(1, 1)
+        load_words(1)
+        load_scales(1)
+        load_y(1, 0)
+        load_y(1, 1)
+        for g in range(4):
+            load_x(1, g)
+        nc.sync.dma_start(out=pw[:], in_=prog_words.rearrange("g p b -> p g b"))
+        for b in range(4):
+            nc.sync.dma_start(out=ps[32 * b : 32 * b + 4, :, :].bitcast(I32), in_=psr[4 * b : 4 * b + 4].bitcast(I32))
+
+        prod_t = {}
+        bank_t = {}
+        group = {}
+        codes = {}
+        scales = {}
+        yg = {}
+        tbank = [0]
+
+        def perm_words(q):
+            nc.vector.tensor_copy(
+                out=w[q][:].rearrange("p g (t m b) -> p g t m b", t=4, b=2),
+                in_=w_raw[q][:].rearrange("p g (m t b) -> p g t m b", t=4, b=2),
+            )
+
+        def perm_scales(q):
+            nc.vector.tensor_copy(
+                out=s[q][:].rearrange("p g (t m) -> p g t m", t=4),
+                in_=s_raw[q][:].rearrange("p g (m t) -> p g t m", t=4),
+            )
+
+        def prod(h, g):
+            t = tile([128, 4, 512], BF16, "prod%d_%d" % (h, g), "prod%d" % g)
+            prod_t[h, g] = t
+            for a in range(4):
+                nc.vector.tensor_tensor(out=t[:, a, :], in0=x[h][g][:, a, :].bitcast(FP8), in1=sc[g][:], op=MULT)
+
+        def trans(h, c):
+            for pair in range(2):
+                j = tbank[0] % 3
+                tbank[0] += 1
+                b = bank(j, "tr%d_%d_%d" % (h, c, pair))
+                bank_t[h, c, pair] = b
+                v = b[:].rearrange("p (u r) -> p u r", u=2)
+                for a in range(2):
+                    src = pn[h][pair][:, a, 512 * c : 512 * c + 512] if c < 2 else prod_t[h, c - 2][:, 2 * pair + a, :]
+                    words = src.bitcast(F32)
+                    for u in range(2):
+                        nc.tensor.transpose(v[:, u, 128 * a : 128 * a + 128], words[:, u:256:2], ident[:])
+
+        def evac(h, c):
+            t = tile([128, 2048], BF16, "grp%d_%d" % (h, c), "grp%d" % c)
+            group[h, c] = t
+            for pair in range(2):
+                nc.scalar.copy(
+                    out=t[:, 1024 * pair : 1024 * pair + 1024].bitcast(F32).rearrange("p (r u) -> p r u", u=2),
+                    in_=bank_t[h, c, pair][:].rearrange("p (u r) -> p r u", u=2),
+                )
+
+        def quant(h, c):
+            codes[h, c] = tile([128, 512], U32, "qc%d_%d" % (h, c))
+            scales[h, c] = tile([128, 512], U8, "qs%d_%d" % (h, c))
+            nc.vector.quantize_mx(out=codes[h, c][:].bitcast(E4M3X4), scales=scales[h, c][:], in_=group[h, c][:])
+
+        def yint(q, g):
+            t = tile([128, 2048], BF16, "yg%d_%d" % (q, g), "yg%d" % g)
+            yg[q, g] = t
+            nc.scalar.copy(
+                out=t[:].rearrange("p (t m j) -> p t m j", t=4, j=4),
+                in_=y_raw[q][g][:].rearrange("p j (m t) -> p t m j", t=4),
+            )
+
+        def yquant(q, g):
+            nc.vector.quantize_mx(out=yc[q][g][:].bitcast(E4M3X4), scales=ys[q][g][:], in_=yg[q, g][:])
+
+        acc = {}
+
+        def mm(h, q, t, c, first, last):
+            if c < 2:
+                lhs = yc[q][c][:, 128 * t : 128 * t + 128].bitcast(E4M3X4)
+                lsc = ys[q][c][:, 128 * t : 128 * t + 128]
+            else:
+                lhs = w[q][:, c - 2, 256 * t : 256 * t + 256].bitcast(E2M1X4)
+                lsc = s[q][:, c - 2, 128 * t : 128 * t + 128]
+            nc.tensor.matmul_mx(
+                out=acc[h, q, t][:], lhsT=lhs, lhsT_scale=lsc,
+                rhs=codes[h, c][:].bitcast(E4M3X4), rhs_scale=scales[h, c][:],
+                start=first, stop=last,
+            )
+
+        def open_acc(h, q, t, j):
+            acc[h, q, t] = bank(j, "acc%d_%d_%d" % (h, q, t))
+
+        planes = {}
+
+        def effect(h, q, t):
+            if t == 0:
+                planes[h, q] = tile([128, 4, 512], BF16, "pl%d_%d" % (h, q), "pl%d" % q)
+            nc.scalar.activation(
+                out=planes[h, q][:, t, :], in_=acc[h, q, t][:], func=ACT.Identity,
+                bias=nb[:, 4 * q + t : 4 * q + t + 1], scale=vecf[:, 1, 4 * q + t : 4 * q + t + 1],
+            )
+
+        eg = {}
+        ec = {}
+        es = {}
+
+        def eint(h, q, m0, m1):
+            if m0 == 0:
+                eg[h, q] = tile([128, 2048], BF16, "eg%d_%d" % (h, q), "eg%d" % q)
+            nc.vector.tensor_copy(
+                out=eg[h, q][:, 4 * m0 : 4 * m1].rearrange("p (m t) -> p m t", t=4),
+                in_=planes[h, q][:, :, m0:m1].rearrange("p t m -> p m t"),
+            )
+
+        def equant(h, q, m0, m1):
+            if m0 == 0:
+                ec[h, q] = tile([128, 512], U32, "ec%d_%d" % (h, q))
+                es[h, q] = tile([128, 512], U8, "es%d_%d" % (h, q))
+            nc.vector.quantize_mx(out=ec[h, q][:, m0:m1].bitcast(E4M3X4), scales=es[h, q][:, m0:m1], in_=eg[h, q][:, 4 * m0 : 4 * m1])
+
+        orow = out.rearrange("(p a) r -> p a r", a=8)
+
+        sbank = {}
+
+        def score_mm(h, a, q, j=None):
+            if q == 0:
+                sbank[h, a] = bank(j, "score%d_%d" % (h, a))
+            c = slice(128 * a, 128 * a + 128)
+            nc.tensor.matmul_mx(
+                out=sbank[h, a][:], lhsT=ec[h, q][:, c].bitcast(E4M3X4), lhsT_scale=es[h, q][:, c],
+                rhs=pw[:, q, :].bitcast(E2M1X4), rhs_scale=ps[:, q, :], start=(q == 0), stop=(q == 1),
+            )
+
+        def score_out(h, a, on_vector=False):
+            t = tile([128, 512], F32, "out%d_%d" % (h, a), "out%d" % a)
+            pcol = vecf[:, 2, 4 * h + a : 4 * h + a + 1]
+            if on_vector:
+                nc.vector.tensor_scalar(out=t[:], in0=sbank[h, a][:], scalar1=pcol, scalar2=None, op0=MULT)
+            else:
+                nc.scalar.activation(out=t[:], in_=sbank[h, a][:], func=ACT.Copy, scale=pcol)
+            nc.sync.dma_start(out=orow[:, 4 * h + a, :], in_=t[:])
+
+        for t in range(4):
+            open_acc(0, 0, t, 3 + t)
+
+        def mms(h, q, c, first=False, last=False):
+            for t in range(4):
+                mm(h, q, t, c, first, last)
+
+        def tile_mms(h, q, t, j, order=(2, 3, 4, 5, 0, 1)):
+            open_acc(h, q, t, j)
+            for i, c in enumerate(order):
+                mm(h, q, t, c, i == 0, i == 5)
+
+        perm_words(0)
+        prod(0, 0)
+        trans(0, 0); evac(0, 0)
+        trans(0, 1); evac(0, 1)
+        trans(0, 2); evac(0, 2)
+        perm_scales(0)
+        prod(0, 1)
+        quant(0, 2)
+        yint(0, 0)
+        trans(0, 3); evac(0, 3)
+        mms(0, 0, 2, first=True)
+        quant(0, 0)
+        prod(0, 2)
+        yint(0, 1)
+        trans(0, 4); evac(0, 4)
+        quant(0, 3)
+        yquant(0, 0)
+        mms(0, 0, 3)
+        mms(0, 0, 0)
+        prod(0, 3)
+        trans(0, 5); evac(0, 5)
+        trans(1, 0); evac(1, 0)
+        quant(0, 4)
+        mms(0, 0, 4)
+        quant(0, 1)
+        yquant(0, 1)
+        mms(0, 0, 1)
+        trans(1, 1); evac(1, 1)
+        quant(0, 5)
+        mms(0, 0, 5, last=True)
+        for t in range(4):
+            effect(0, 0, t)
+        yint(1, 0)
+        yint(1, 1)
+        perm_words(1)
+        perm_scales(1)
+        prod(1, 0)
+        trans(1, 2); evac(1, 2)
+
+        yquant(1, 0)
+        quant(1, 0)
+        yquant(1, 1)
+        prod(1, 1)
+        tile_mms(0, 1, 0, 3)
+        effect(0, 1, 0)
+        quant(1, 1)
+        quant(1, 2)
+        trans(1, 3); evac(1, 3)
+        tile_mms(0, 1, 1, 4)
+        effect(0, 1, 1)
+        prod(1, 2)
+        eint(0, 0, 0, 512)
+        quant(1, 3)
+        trans(1, 4); evac(1, 4)
+        tile_mms(0, 1, 2, 5)
+        effect(0, 1, 2)
+        prod(1, 3)
+        equant(0, 0, 0, 512)
+        quant(1, 4)
+        trans(1, 5); evac(1, 5)
+        tile_mms(0, 1, 3, 6)
+        effect(0, 1, 3)
+        for t in range(4):
+            open_acc(1, 0, t, 3 + t)
+        mms(1, 0, 2, first=True)
+        mms(1, 0, 0)
+        mms(1, 0, 1)
+        quant(1, 5)
+        mms(1, 0, 3)
+        mms(1, 0, 4)
+        mms(1, 0, 5, last=True)
+        eint(0, 1, 0, 512)
+        equant(0, 1, 0, 512)
+        for t in range(4):
+            effect(1, 0, t)
+        for t in range(4):
+            tile_mms(1, 1, t, [1, 2, 7, 0][t])
+            effect(1, 1, t)
+            if t == 1:
+                eint(1, 0, 0, 512)
+                equant(1, 0, 0, 512)
+                for a in range(2):
+                    score_mm(0, a, 0, 3 + a)
+                    score_mm(0, a, 1)
+                    score_out(0, a)
+        for a in range(2, 4):
+            score_mm(0, a, 0, 3 + a)
+            score_mm(0, a, 1)
+        for m0 in (0, 256):
+            eint(1, 1, m0, m0 + 256)
+            equant(1, 1, m0, m0 + 256)
+        for a in range(4):
+            score_mm(1, a, 0, [3, 4, 1, 2][a])
+        for a in range(2, 4):
+            score_out(0, a)
+        for a in range(4):
+            score_mm(1, a, 1)
+            score_out(1, a, on_vector=(a % 2 == 1))

@@ -3,361 +3,406 @@ from contextlib import ExitStack
 import concourse.mybir as mybir
 from concourse.masks import make_identity
 
-M, C1, C2, N, R = 1024, 1024, 2048, 1024, 512
-FLOPS = 2 * M * N * (C1 + C2) + 2 * M * N * R
+PERTURBATIONS, NEW, OLD, GENES, PROGRAMMES = 1024, 1024, 2048, 1024, 512
+FLOPS = 2 * PERTURBATIONS * GENES * (NEW + OLD) + 2 * PERTURBATIONS * GENES * PROGRAMMES
 
 F32 = mybir.dt.float32
 BF16 = mybir.dt.bfloat16
 U32 = mybir.dt.uint32
 I32 = mybir.dt.int32
 U8 = mybir.dt.uint8
-FP8 = mybir.dt.float8_e4m3fn
+E4M3FN = mybir.dt.float8_e4m3fn
 E4M3X4 = mybir.dt.float8_e4m3fn_x4
 E2M1X4 = mybir.dt.float4_e2m1fn_x4
 MULT = mybir.AluOpType.mult
 ADD = mybir.AluOpType.add
-ACT = mybir.ActivationFunctionType
+SUB = mybir.AluOpType.subtract
+COPY = mybir.ActivationFunctionType.Copy
+IDENTITY = mybir.ActivationFunctionType.Identity
+
+P = 128
+J = 4
+K = P * J
+NEW_PASSES = (0, 1)
+OLD_PASSES = (2, 3, 4, 5)
+PASSES = len(NEW_PASSES) + len(OLD_PASSES)
+BANKS = 8
+CLOCK_MATMULS = 20
 
 
 def tile_perturb_seq_programmes_s3_kernel(
-    tc, pinv_new, pinv_old_bytes, pinv_old_scale, y_new, old_words, old_scales,
-    control, inv_sd, prog_words, prog_scales, precision, out,
+    tc,
+    pinv_new,
+    pinv_old_bytes,
+    pinv_old_scale,
+    y_new,
+    old_words,
+    old_scales,
+    control,
+    inv_sd,
+    prog_words,
+    prog_scales,
+    precision,
+    out,
 ):
     nc = tc.nc
     with ExitStack() as ctx:
-        sb = ctx.enter_context(tc.tile_pool(name="sb", bufs=1))
+        sbuf = ctx.enter_context(tc.tile_pool(name="sbuf", bufs=1))
         psum = ctx.enter_context(tc.psum_pool(name="psum", bufs=1))
         ctx.enter_context(tc.manual_schedule())
 
         def tile(shape, dtype, name, tag=None):
-            return sb.tile(shape, dtype, name=name, tag=tag or name, align_bytes=64)
+            return sbuf.tile(shape, dtype, name=name, tag=tag or name, align_bytes=64)
 
-        def bank(j, name):
-            return psum.tile([128, 512], F32, name=name, tag="bank%d" % j)
+        free_banks = list(range(BANKS))
+        bank_of = {}
 
-        ident = tile([128, 128], F32, "ident")
-        w_raw = [tile([128, 4, 1024], U8, "w_raw%d" % q) for q in range(2)]
-        w = [tile([128, 4, 1024], U8, "w%d" % q) for q in range(2)]
-        s_raw = [tile([128, 4, 512], U8, "s_raw%d" % q) for q in range(2)]
-        s = [tile([128, 4, 512], U8, "s%d" % q) for q in range(2)]
-        pw = tile([128, 2, 1024], U8, "pw")
-        ps = tile([128, 2, 512], U8, "ps")
-        sc = [tile([128, 512], F32, "sc%d" % g) for g in range(4)]
-        x = [[tile([128, 4, 512], U8, "x%d%d" % (h, g)) for g in range(4)] for h in range(2)]
-        pn = [[tile([128, 2, 1024], BF16, "pn%d%d" % (h, i)) for i in range(2)] for h in range(2)]
-        y_raw = [[tile([128, 4, 512], BF16, "y_raw%d%d" % (q, g)) for g in range(2)] for q in range(2)]
-        yc = [[tile([128, 512], U32, "yc%d%d" % (q, g)) for g in range(2)] for q in range(2)]
-        ys = [[tile([128, 512], U8, "ys%d%d" % (q, g)) for g in range(2)] for q in range(2)]
-        vec = [tile([128, 8], BF16, "vec%d" % i) for i in range(3)]
-        vecf = tile([128, 3, 8], F32, "vecf")
-        nb0 = tile([128, 8], F32, "nb0")
-        nb = tile([128, 8], F32, "nb")
-        dummy = tile([128, 1], F32, "dummy")
+        def take_bank(key, name):
+            j = free_banks.pop(0)
+            bank_of[key] = (j, psum.tile([P, 512], F32, name=name, tag="bank%d" % j))
+            return bank_of[key][1]
 
-        nc.gpsimd.memset(s_raw[0][:].rearrange("p g n -> p (g n)").bitcast(I32), 0)
-        nc.gpsimd.memset(s_raw[1][:].rearrange("p g n -> p (g n)").bitcast(I32), 0)
-        nc.gpsimd.memset(ps[:].rearrange("p g n -> p (g n)").bitcast(I32), 0)
+        def last_use(key):
+            free_banks.append(bank_of[key][0])
+            return bank_of[key][1]
+
+        ident = tile([P, P], F32, "ident")
+        zeros = tile([P, 512], BF16, "zeros")
+        scale_cols = tile([P, 16], F32, "scale_cols")
+        scale_rows = tile([P, OLD], F32, "scale_rows")
+        bytes0 = [tile([P, 4, 1024], U8, "bytes0_%d" % i) for i in range(2)]
+        bytes1 = [tile([P, 2, OLD], U8, "bytes1_%d" % i) for i in range(2)]
+        new_rows = [[tile([P, 2, NEW], BF16, "new_rows%d_%d" % (h, i)) for i in range(2)] for h in range(2)]
+        y_raw = [[tile([P, J, 512], BF16, "y_raw%d_%d" % (q, c)) for c in NEW_PASSES] for q in range(2)]
+        y_codes = [[tile([P, 512], U32, "y_codes%d_%d" % (q, c)) for c in NEW_PASSES] for q in range(2)]
+        y_scales = [[tile([P, 512], U8, "y_scales%d_%d" % (q, c)) for c in NEW_PASSES] for q in range(2)]
+        words_raw = [tile([P, 2, 2 * GENES], U8, "words_raw%d" % i) for i in range(2)]
+        words = [[tile([P, 2, 1024], U8, "words%d_%d" % (q, i)) for i in range(2)] for q in range(2)]
+        w_scales_raw = tile([P, 4, GENES], U8, "w_scales_raw")
+        w_scales = [tile([P, 4, 512], U8, "w_scales%d" % q) for q in range(2)]
+        v_words = tile([P, 2, 2 * PROGRAMMES], U8, "v_words")
+        v_scales = tile([P, 2, PROGRAMMES], U8, "v_scales")
+        ctl_in, isd_in, prec_in = (tile([P, 8], BF16, n) for n in ("ctl_in", "isd_in", "prec_in"))
+        ctl, isd, prec = (tile([P, 8], F32, n) for n in ("ctl", "isd", "prec"))
+        ctl_isd = tile([P, 8], F32, "ctl_isd")
+        minus_ctl_isd = tile([P, 8], F32, "minus_ctl_isd")
+        table_load = tile([P, 1], F32, "table_load")
+
         make_identity(nc, ident[:])
-        nc.gpsimd.dma_start(out=vec[0][:].rearrange("p (g t) -> p g t", t=4), in_=control.rearrange("(g p t) -> p g t", p=128, t=4))
-        nc.gpsimd.dma_start(out=vec[1][:].rearrange("p (g t) -> p g t", t=4), in_=inv_sd.rearrange("(g p t) -> p g t", p=128, t=4))
-        nc.gpsimd.dma_start(out=vec[2][:], in_=precision.rearrange("(p a) -> p a", a=8))
-        for i in range(3):
-            nc.gpsimd.tensor_copy(out=vecf[:, i, :], in_=vec[i][:])
-        nc.gpsimd.tensor_tensor(out=nb0[:], in0=vecf[:, 0, :], in1=vecf[:, 1, :], op=MULT)
-        nc.gpsimd.tensor_scalar(out=nb[:], in0=nb0[:], scalar1=-1.0, scalar2=0.0, op0=MULT, op1=ADD)
-        nc.vector.memset(dummy[:], 0.0)
-        nc.scalar.activation(out=dummy[:], in_=dummy[:], func=ACT.Identity)
+        nc.vector.memset(w_scales_raw[:].rearrange("p g n -> p (g n)").bitcast(I32), 0)
+        nc.gpsimd.memset(v_scales[:].rearrange("p g n -> p (g n)").bitcast(I32), 0)
+        for vec, src in ((control, ctl_in), (inv_sd, isd_in)):
+            nc.gpsimd.dma_start(out=src[:].rearrange("p (q t) -> p q t", t=J), in_=vec.rearrange("(q p t) -> p q t", p=P, t=J))
+        nc.gpsimd.dma_start(out=prec_in[:], in_=precision.rearrange("(p a) -> p a", a=8))
+        for dst, src in ((ctl, ctl_in), (isd, isd_in), (prec, prec_in)):
+            nc.gpsimd.tensor_copy(out=dst[:], in_=src[:])
+        nc.gpsimd.tensor_tensor(out=ctl_isd[:], in0=ctl[:], in1=isd[:], op=MULT)
+        nc.gpsimd.tensor_scalar(out=minus_ctl_isd[:], in0=ctl_isd[:], scalar1=-1.0, scalar2=0.0, op0=MULT, op1=ADD)
 
-        xr = pinv_old_bytes.rearrange("(p a) k -> p a k", a=8)
-        pr = pinv_new.rearrange("(p a) k -> p a k", a=8)
-        sr = old_scales.rearrange("g r n -> r g n")
-        psr = prog_scales.rearrange("g r n -> r g n")
+        nc.vector.memset(zeros[:], 0.0)
+        nc.vector.memset(table_load[:], 0.0)
+        nc.scalar.activation(out=table_load[:], in_=table_load[:], func=IDENTITY)
 
-        def load_words(q):
-            c = slice(1024 * q, 1024 * q + 1024)
-            nc.sync.dma_start(out=w_raw[q][:], in_=old_words[:, :, c].rearrange("g p b -> p g b"))
+        byte_rows = pinv_old_bytes.rearrange("(p a) k -> p a k", a=8)
+        cell_rows = pinv_new.rearrange("(p a) k -> p a k", a=8)
 
-        def load_y(q, g):
-            nc.sync.dma_start(out=y_raw[q][g][:], in_=y_new[512 * g : 512 * g + 512, 512 * q : 512 * q + 512].rearrange("(p j) n -> p j n", j=4))
-
-        def load_sc(g):
-            nc.sync.dma_start(out=sc[g][:], in_=pinv_old_scale[:, 512 * g : 512 * g + 512].rearrange("o k -> (o k)").partition_broadcast(128))
-
-        def load_x(h, g):
-            nc.sync.dma_start(out=x[h][g][:], in_=xr[:, 4 * h : 4 * h + 4, 512 * g : 512 * g + 512])
-
-        def load_pn(h, i):
-            nc.sync.dma_start(out=pn[h][i][:], in_=pr[:, 4 * h + 2 * i : 4 * h + 2 * i + 2, :])
-
-        def load_scales(q):
+        def load_scale_bytes(dst, src):
+            rows = src.rearrange("g r n -> r g n")
             for b in range(4):
-                nc.sync.dma_start(out=s_raw[q][32 * b : 32 * b + 4, :, :].bitcast(I32), in_=sr[4 * b : 4 * b + 4, :, 512 * q : 512 * q + 512].bitcast(I32))
+                nc.sync.dma_start(out=dst[32 * b : 32 * b + 4, :, :].bitcast(I32), in_=rows[4 * b : 4 * b + 4].bitcast(I32))
 
-        load_words(0)
-        load_sc(0)
-        load_x(0, 0)
-        load_scales(0)
-        load_pn(0, 0)
-        load_pn(0, 1)
-        load_sc(1)
-        load_x(0, 1)
+        def load_new_rows(h, i):
+            nc.sync.dma_start(out=new_rows[h][i][:], in_=cell_rows[:, 4 * h + 2 * i : 4 * h + 2 * i + 2, :])
+
+        def load_y(q, c):
+            src = y_new[K * c : K * c + K, 512 * q : 512 * q + 512]
+            nc.sync.dma_start(out=y_raw[q][c][:], in_=src.rearrange("(p j) n -> p j n", j=J))
+
+        def load_words(i):
+            nc.sync.dma_start(out=words_raw[i][:], in_=old_words[2 * i : 2 * i + 2].rearrange("g p b -> p g b"))
+
+        nc.sync.dma_start(out=scale_cols[:], in_=pinv_old_scale.rearrange("o (n m) -> (o n) m", m=16))
+        load_new_rows(0, 0)
+        load_scale_bytes(w_scales_raw, old_scales)
+        nc.sync.dma_start(out=bytes0[0][:], in_=byte_rows[:, 0:4, 0:1024])
+        load_new_rows(0, 1)
         load_y(0, 0)
-        load_sc(2)
-        load_x(0, 2)
-        load_y(0, 1)
-        load_sc(3)
-        load_x(0, 3)
-        load_pn(1, 0)
-        load_pn(1, 1)
-        load_words(1)
-        load_scales(1)
+        nc.sync.dma_start(out=bytes0[1][:], in_=byte_rows[:, 0:4, 1024:2048])
+        load_words(0)
         load_y(1, 0)
+        load_new_rows(1, 0)
+        load_new_rows(1, 1)
+        load_y(0, 1)
+        load_words(1)
+        for i in range(2):
+            nc.sync.dma_start(out=bytes1[i][:], in_=byte_rows[:, 4 + 2 * i : 6 + 2 * i, :])
         load_y(1, 1)
-        for g in range(4):
-            load_x(1, g)
-        nc.sync.dma_start(out=pw[:], in_=prog_words.rearrange("g p b -> p g b"))
-        for b in range(4):
-            nc.sync.dma_start(out=ps[32 * b : 32 * b + 4, :, :].bitcast(I32), in_=psr[4 * b : 4 * b + 4].bitcast(I32))
+        load_scale_bytes(v_scales, prog_scales)
+        nc.sync.dma_start(out=v_words[:], in_=prog_words.rearrange("g p b -> p g b"))
 
-        prod_t = {}
-        bank_t = {}
-        group = {}
-        codes = {}
-        scales = {}
-        yg = {}
-        tbank = [0]
+        clock_done = []
 
-        def perm_words(q):
+        def keep_clock(n):
+            for i in range(n):
+                if not clock_done:
+                    take_bank("clock", "clock")
+                clock_done.append(i)
+                nc.tensor.matmul(bank_of["clock"][1][:], lhsT=zeros[:, 0:P], rhs=zeros[:], start=True, stop=True)
+            if len(clock_done) == CLOCK_MATMULS:
+                last_use("clock")
+
+        def spread_scales():
+            for i in range(4):
+                b = take_bank(("spread", i), "spread%d" % i)
+                for m in range(4):
+                    col = scale_cols[:, 4 * i + m : 4 * i + m + 1].to_broadcast([P, P])
+                    nc.tensor.transpose(b[:, P * m : P * m + P], col, ident[:])
+            by_cell = scale_rows[:].rearrange("p (n m) -> p n m", m=16)
+            for i in range(4):
+                nc.scalar.copy(out=by_cell[:, :, 4 * i : 4 * i + 4], in_=last_use(("spread", i))[:].rearrange("p (m n) -> p n m", m=4))
+
+        def permute_words(i, q):
             nc.vector.tensor_copy(
-                out=w[q][:].rearrange("p g (t m b) -> p g t m b", t=4, b=2),
-                in_=w_raw[q][:].rearrange("p g (m t b) -> p g t m b", t=4, b=2),
+                out=words[q][i][:].rearrange("p g (t m b) -> p g t m b", t=J, b=2),
+                in_=words_raw[i][:, :, 1024 * q : 1024 * q + 1024].rearrange("p g (m t b) -> p g t m b", t=J, b=2),
             )
 
-        def perm_scales(q):
+        def permute_scale_bytes(q):
             nc.vector.tensor_copy(
-                out=s[q][:].rearrange("p g (t m) -> p g t m", t=4),
-                in_=s_raw[q][:].rearrange("p g (m t) -> p g t m", t=4),
+                out=w_scales[q][:].rearrange("p g (t m) -> p g t m", t=J),
+                in_=w_scales_raw[:, :, 512 * q : 512 * q + 512].rearrange("p g (m t) -> p g t m", t=J),
             )
 
-        def prod(h, g):
-            t = tile([128, 4, 512], BF16, "prod%d_%d" % (h, g), "prod%d" % g)
-            prod_t[h, g] = t
-            for a in range(4):
-                nc.vector.tensor_tensor(out=t[:, a, :], in0=x[h][g][:, a, :].bitcast(FP8), in1=sc[g][:], op=MULT)
+        widened = {}
 
-        def trans(h, c):
-            for pair in range(2):
-                j = tbank[0] % 3
-                tbank[0] += 1
-                b = bank(j, "tr%d_%d_%d" % (h, c, pair))
-                bank_t[h, c, pair] = b
-                v = b[:].rearrange("p (u r) -> p u r", u=2)
+        def widen(h, g):
+            scale = scale_rows[:, K * g : K * g + K]
+            for i in range(2):
+                widened[h, g, i] = tile([P, 2, K], BF16, "widened%d_%d_%d" % (h, g, i), "widened%d_%d" % (g, i))
                 for a in range(2):
-                    src = pn[h][pair][:, a, 512 * c : 512 * c + 512] if c < 2 else prod_t[h, c - 2][:, 2 * pair + a, :]
-                    words = src.bitcast(F32)
-                    for u in range(2):
-                        nc.tensor.transpose(v[:, u, 128 * a : 128 * a + 128], words[:, u:256:2], ident[:])
+                    src = bytes0[g // 2][:, 2 * i + a, K * (g % 2) : K * (g % 2) + K] if h == 0 else bytes1[i][:, a, K * g : K * g + K]
+                    nc.vector.tensor_tensor(out=widened[h, g, i][:, a, :], in0=src.bitcast(E4M3FN), in1=scale, op=MULT)
 
-        def evac(h, c):
-            t = tile([128, 2048], BF16, "grp%d_%d" % (h, c), "grp%d" % c)
-            group[h, c] = t
-            for pair in range(2):
+        def turn(h, c):
+            for i in range(2):
+                b = take_bank(("turn", h, c, i), "turn%d_%d_%d" % (h, c, i))
+                by_word = b[:].rearrange("p (u r) -> p u r", u=2)
+                for a in range(2):
+                    rows = new_rows[h][i][:, a, K * c : K * c + K] if c in NEW_PASSES else widened[h, c - 2, i][:, a, :]
+                    pairs = rows.bitcast(F32)
+                    for u in range(2):
+                        nc.tensor.transpose(by_word[:, u, P * a : P * a + P], pairs[:, u : K // 2 : 2], ident[:])
+
+        grouped = {}
+
+        def regroup(h, c):
+            grouped[h, c] = tile([P, 4 * 512], BF16, "grouped%d_%d" % (h, c), "grouped%d" % c)
+            for i in range(2):
                 nc.scalar.copy(
-                    out=t[:, 1024 * pair : 1024 * pair + 1024].bitcast(F32).rearrange("p (r u) -> p r u", u=2),
-                    in_=bank_t[h, c, pair][:].rearrange("p (u r) -> p r u", u=2),
+                    out=grouped[h, c][:, 1024 * i : 1024 * i + 1024].bitcast(F32).rearrange("p (r u) -> p r u", u=2),
+                    in_=last_use(("turn", h, c, i))[:].rearrange("p (u r) -> p r u", u=2),
                 )
 
-        def quant(h, c):
-            codes[h, c] = tile([128, 512], U32, "qc%d_%d" % (h, c))
-            scales[h, c] = tile([128, 512], U8, "qs%d_%d" % (h, c))
-            nc.vector.quantize_mx(out=codes[h, c][:].bitcast(E4M3X4), scales=scales[h, c][:], in_=group[h, c][:])
+        codes, code_scales = {}, {}
 
-        def yint(q, g):
-            t = tile([128, 2048], BF16, "yg%d_%d" % (q, g), "yg%d" % g)
-            yg[q, g] = t
+        def quantize_rows(h, c):
+            codes[h, c] = tile([P, 512], U32, "codes%d_%d" % (h, c))
+            code_scales[h, c] = tile([P, 512], U8, "code_scales%d_%d" % (h, c))
+            nc.vector.quantize_mx(out=codes[h, c][:].bitcast(E4M3X4), scales=code_scales[h, c][:], in_=grouped[h, c][:])
+
+        y_grouped = {}
+
+        def interleave_y(q, c):
+            y_grouped[q, c] = tile([P, 4 * 512], BF16, "y_grouped%d_%d" % (q, c), "y_grouped%d" % c)
             nc.scalar.copy(
-                out=t[:].rearrange("p (t m j) -> p t m j", t=4, j=4),
-                in_=y_raw[q][g][:].rearrange("p j (m t) -> p t m j", t=4),
+                out=y_grouped[q, c][:].rearrange("p (t m j) -> p m t j", t=J, j=J),
+                in_=y_raw[q][c][:].rearrange("p j (m t) -> p m t j", t=J),
             )
 
-        def yquant(q, g):
-            nc.vector.quantize_mx(out=yc[q][g][:].bitcast(E4M3X4), scales=ys[q][g][:], in_=yg[q, g][:])
+        def quantize_y(q, c):
+            nc.vector.quantize_mx(out=y_codes[q][c][:].bitcast(E4M3X4), scales=y_scales[q][c][:], in_=y_grouped[q, c][:])
 
-        acc = {}
+        passes_added = {}
 
-        def mm(h, q, t, c, first, last):
-            if c < 2:
-                lhs = yc[q][c][:, 128 * t : 128 * t + 128].bitcast(E4M3X4)
-                lsc = ys[q][c][:, 128 * t : 128 * t + 128]
+        def add_pass(h, q, t, c):
+            key = (h, q, t)
+            n = passes_added.get(key, 0)
+            passes_added[key] = n + 1
+            acc = take_bank(key, "acc%d_%d_%d" % key) if n == 0 else bank_of[key][1]
+            if c in NEW_PASSES:
+                cols = slice(P * t, P * t + P)
+                lhs, lhs_scale = y_codes[q][c][:, cols].bitcast(E4M3X4), y_scales[q][c][:, cols]
             else:
-                lhs = w[q][:, c - 2, 256 * t : 256 * t + 256].bitcast(E2M1X4)
-                lsc = s[q][:, c - 2, 128 * t : 128 * t + 128]
+                g = c - 2
+                lhs = words[q][g // 2][:, g % 2, 2 * P * t : 2 * P * t + 2 * P].bitcast(E2M1X4)
+                lhs_scale = w_scales[q][:, g, P * t : P * t + P]
             nc.tensor.matmul_mx(
-                out=acc[h, q, t][:], lhsT=lhs, lhsT_scale=lsc,
-                rhs=codes[h, c][:].bitcast(E4M3X4), rhs_scale=scales[h, c][:],
-                start=first, stop=last,
+                out=acc[:],
+                lhsT=lhs,
+                lhsT_scale=lhs_scale,
+                rhs=codes[h, c][:].bitcast(E4M3X4),
+                rhs_scale=code_scales[h, c][:],
+                start=(n == 0),
+                stop=(n == PASSES - 1),
             )
 
-        def open_acc(h, q, t, j):
-            acc[h, q, t] = bank(j, "acc%d_%d_%d" % (h, q, t))
+        def add_passes(h, q, ts, cs):
+            for c in cs:
+                for t in ts:
+                    add_pass(h, q, t, c)
 
-        planes = {}
+        effect = {}
 
-        def effect(h, q, t):
-            if t == 0:
-                planes[h, q] = tile([128, 4, 512], BF16, "pl%d_%d" % (h, q), "pl%d" % q)
-            nc.scalar.activation(
-                out=planes[h, q][:, t, :], in_=acc[h, q, t][:], func=ACT.Identity,
-                bias=nb[:, 4 * q + t : 4 * q + t + 1], scale=vecf[:, 1, 4 * q + t : 4 * q + t + 1],
-            )
-
-        eg = {}
-        ec = {}
-        es = {}
-
-        def eint(h, q, m0, m1):
-            if m0 == 0:
-                eg[h, q] = tile([128, 2048], BF16, "eg%d_%d" % (h, q), "eg%d" % q)
-            nc.vector.tensor_copy(
-                out=eg[h, q][:, 4 * m0 : 4 * m1].rearrange("p (m t) -> p m t", t=4),
-                in_=planes[h, q][:, :, m0:m1].rearrange("p t m -> p m t"),
-            )
-
-        def equant(h, q, m0, m1):
-            if m0 == 0:
-                ec[h, q] = tile([128, 512], U32, "ec%d_%d" % (h, q))
-                es[h, q] = tile([128, 512], U8, "es%d_%d" % (h, q))
-            nc.vector.quantize_mx(out=ec[h, q][:, m0:m1].bitcast(E4M3X4), scales=es[h, q][:, m0:m1], in_=eg[h, q][:, 4 * m0 : 4 * m1])
-
-        orow = out.rearrange("(p a) r -> p a r", a=8)
-
-        sbank = {}
-
-        def score_mm(h, a, q, j=None):
-            if q == 0:
-                sbank[h, a] = bank(j, "score%d_%d" % (h, a))
-            c = slice(128 * a, 128 * a + 128)
-            nc.tensor.matmul_mx(
-                out=sbank[h, a][:], lhsT=ec[h, q][:, c].bitcast(E4M3X4), lhsT_scale=es[h, q][:, c],
-                rhs=pw[:, q, :].bitcast(E2M1X4), rhs_scale=ps[:, q, :], start=(q == 0), stop=(q == 1),
-            )
-
-        def score_out(h, a, on_vector=False):
-            t = tile([128, 512], F32, "out%d_%d" % (h, a), "out%d" % a)
-            pcol = vecf[:, 2, 4 * h + a : 4 * h + a + 1]
-            if on_vector:
-                nc.vector.tensor_scalar(out=t[:], in0=sbank[h, a][:], scalar1=pcol, scalar2=None, op0=MULT)
+        def finish_effect(h, q, t, on=nc.scalar):
+            if (h, q) not in effect:
+                effect[h, q] = tile([P, J, 512], BF16, "effect%d_%d" % (h, q), "effect%d" % q)
+            acc = last_use((h, q, t))
+            col = slice(4 * q + t, 4 * q + t + 1)
+            if on is nc.scalar:
+                nc.scalar.activation(out=effect[h, q][:, t, :], in_=acc[:], func=IDENTITY, bias=minus_ctl_isd[:, col], scale=isd[:, col])
             else:
-                nc.scalar.activation(out=t[:], in_=sbank[h, a][:], func=ACT.Copy, scale=pcol)
-            nc.sync.dma_start(out=orow[:, 4 * h + a, :], in_=t[:])
+                nc.vector.tensor_scalar(out=effect[h, q][:, t, :], in0=acc[:], scalar1=ctl[:, col], scalar2=isd[:, col], op0=SUB, op1=MULT)
 
-        for t in range(4):
-            open_acc(0, 0, t, 3 + t)
+        e_grouped, e_codes, e_scales = {}, {}, {}
 
-        def mms(h, q, c, first=False, last=False):
-            for t in range(4):
-                mm(h, q, t, c, first, last)
+        def interleave_effect(h, q, r0=0, r1=512, on=nc.scalar):
+            if (h, q) not in e_grouped:
+                e_grouped[h, q] = tile([P, 4 * 512], BF16, "e_grouped%d_%d" % (h, q), "e_grouped%d" % q)
+                e_codes[h, q] = tile([P, 512], U32, "e_codes%d_%d" % (h, q))
+                e_scales[h, q] = tile([P, 512], U8, "e_scales%d_%d" % (h, q))
+            copy = nc.scalar.copy if on is nc.scalar else nc.vector.tensor_copy
+            copy(
+                out=e_grouped[h, q][:, J * r0 : J * r1].rearrange("p (r t) -> p r t", t=J),
+                in_=effect[h, q][:, :, r0:r1].rearrange("p t r -> p r t"),
+            )
 
-        def tile_mms(h, q, t, j, order=(2, 3, 4, 5, 0, 1)):
-            open_acc(h, q, t, j)
-            for i, c in enumerate(order):
-                mm(h, q, t, c, i == 0, i == 5)
+        def quantize_effect(h, q, r0=0, r1=512):
+            nc.vector.quantize_mx(
+                out=e_codes[h, q][:, r0:r1].bitcast(E4M3X4), scales=e_scales[h, q][:, r0:r1], in_=e_grouped[h, q][:, J * r0 : J * r1]
+            )
 
-        perm_words(0)
-        prod(0, 0)
-        trans(0, 0); evac(0, 0)
-        trans(0, 1); evac(0, 1)
-        trans(0, 2); evac(0, 2)
-        perm_scales(0)
-        prod(0, 1)
-        quant(0, 2)
-        yint(0, 0)
-        trans(0, 3); evac(0, 3)
-        mms(0, 0, 2, first=True)
-        quant(0, 0)
-        prod(0, 2)
-        yint(0, 1)
-        trans(0, 4); evac(0, 4)
-        quant(0, 3)
-        yquant(0, 0)
-        mms(0, 0, 3)
-        mms(0, 0, 0)
-        prod(0, 3)
-        trans(0, 5); evac(0, 5)
-        trans(1, 0); evac(1, 0)
-        quant(0, 4)
-        mms(0, 0, 4)
-        quant(0, 1)
-        yquant(0, 1)
-        mms(0, 0, 1)
-        trans(1, 1); evac(1, 1)
-        quant(0, 5)
-        mms(0, 0, 5, last=True)
-        for t in range(4):
-            effect(0, 0, t)
-        yint(1, 0)
-        yint(1, 1)
-        perm_words(1)
-        perm_scales(1)
-        prod(1, 0)
-        trans(1, 2); evac(1, 2)
+        def score(h, a, q):
+            b = take_bank(("score", h, a), "score%d_%d" % (h, a)) if q == 0 else bank_of["score", h, a][1]
+            cols = slice(P * a, P * a + P)
+            nc.tensor.matmul_mx(
+                out=b[:],
+                lhsT=e_codes[h, q][:, cols].bitcast(E4M3X4),
+                lhsT_scale=e_scales[h, q][:, cols],
+                rhs=v_words[:, q, :].bitcast(E2M1X4),
+                rhs_scale=v_scales[:, q, :],
+                start=(q == 0),
+                stop=(q == 1),
+            )
 
-        yquant(1, 0)
-        quant(1, 0)
-        yquant(1, 1)
-        prod(1, 1)
-        tile_mms(0, 1, 0, 3)
-        effect(0, 1, 0)
-        quant(1, 1)
-        quant(1, 2)
-        trans(1, 3); evac(1, 3)
-        tile_mms(0, 1, 1, 4)
-        effect(0, 1, 1)
-        prod(1, 2)
-        eint(0, 0, 0, 512)
-        quant(1, 3)
-        trans(1, 4); evac(1, 4)
-        tile_mms(0, 1, 2, 5)
-        effect(0, 1, 2)
-        prod(1, 3)
-        equant(0, 0, 0, 512)
-        quant(1, 4)
-        trans(1, 5); evac(1, 5)
-        tile_mms(0, 1, 3, 6)
-        effect(0, 1, 3)
-        for t in range(4):
-            open_acc(1, 0, t, 3 + t)
-        mms(1, 0, 2, first=True)
-        mms(1, 0, 0)
-        mms(1, 0, 1)
-        quant(1, 5)
-        mms(1, 0, 3)
-        mms(1, 0, 4)
-        mms(1, 0, 5, last=True)
-        eint(0, 1, 0, 512)
-        equant(0, 1, 0, 512)
-        for t in range(4):
-            effect(1, 0, t)
-        for t in range(4):
-            tile_mms(1, 1, t, [1, 2, 7, 0][t])
-            effect(1, 1, t)
-            if t == 1:
-                eint(1, 0, 0, 512)
-                equant(1, 0, 0, 512)
-                for a in range(2):
-                    score_mm(0, a, 0, 3 + a)
-                    score_mm(0, a, 1)
-                    score_out(0, a)
-        for a in range(2, 4):
-            score_mm(0, a, 0, 3 + a)
-            score_mm(0, a, 1)
-        for m0 in (0, 256):
-            eint(1, 1, m0, m0 + 256)
-            equant(1, 1, m0, m0 + 256)
+        out_rows = out.rearrange("(p a) r -> p a r", a=8)
+
+        def finish_score(h, a, on=nc.scalar):
+            b = last_use(("score", h, a))
+            result = tile([P, PROGRAMMES], F32, "result%d_%d" % (h, a))
+            factor = prec[:, 4 * h + a : 4 * h + a + 1]
+            if on is nc.scalar:
+                nc.scalar.activation(out=result[:], in_=b[:], func=COPY, scale=factor)
+            else:
+                nc.vector.tensor_scalar(out=result[:], in0=b[:], scalar1=factor, scalar2=None, op0=MULT)
+            nc.sync.dma_start(out=out_rows[:, 4 * h + a, :], in_=result[:])
+
+        ALL = range(4)
+
+        keep_clock(6)
+        spread_scales()
+        keep_clock(4)
+        for g in range(4):
+            widen(0, g)
+        for c in range(PASSES):
+            turn(0, c)
+            if c < PASSES - 1:
+                keep_clock(2)
+            regroup(0, c)
+            if c == 0:
+                interleave_y(0, 0)
+        turn(1, 0)
+
+        quantize_y(0, 0)
+        quantize_rows(0, 0)
+        interleave_y(1, 0)
+        interleave_y(0, 1)
+        add_passes(0, 0, ALL, (0,))
+        quantize_rows(0, 2)
+        permute_scale_bytes(0)
+        permute_words(0, 0)
+        add_passes(0, 0, ALL, (2,))
+        quantize_rows(0, 3)
+        quantize_rows(0, 4)
+        permute_words(1, 0)
+        quantize_rows(0, 5)
+        quantize_rows(0, 1)
+        turn(1, 1)
+        regroup(1, 0)
+        regroup(1, 1)
+        add_passes(0, 0, ALL, (3, 4))
+        widen(1, 0)
+        quantize_y(0, 1)
+        interleave_y(1, 1)
+        turn(1, 2)
+        regroup(1, 2)
+        add_passes(0, 0, ALL, (5, 1))
+        for t in ALL:
+            finish_effect(0, 0, t)
+
+        quantize_y(1, 0)
+        widen(1, 1)
+        quantize_y(1, 1)
+        add_passes(0, 1, (0, 1), NEW_PASSES)
+        turn(1, 3)
+        regroup(1, 3)
+        permute_scale_bytes(1)
+        permute_words(0, 1)
+        add_passes(0, 1, (2, 3), NEW_PASSES)
+        quantize_rows(1, 2)
+        permute_words(1, 1)
+        interleave_effect(0, 0)
+        add_passes(0, 1, (0, 1), OLD_PASSES)
+        add_passes(0, 1, (2, 3), OLD_PASSES)
+        for c in (3, 0, 1):
+            quantize_rows(1, c)
+        widen(1, 2)
+        widen(1, 3)
+        finish_effect(0, 1, 0)
+        finish_effect(0, 1, 1)
+        turn(1, 4)
+        regroup(1, 4)
+        finish_effect(0, 1, 2)
+        finish_effect(0, 1, 3)
+
+        add_passes(1, 0, ALL, (2, 3))
+        quantize_rows(1, 4)
+        quantize_effect(0, 0)
+        turn(1, 5)
+        regroup(1, 5)
+        interleave_effect(0, 1)
+        quantize_rows(1, 5)
+        add_passes(1, 0, ALL, (0, 1, 4, 5))
+        finish_effect(1, 0, 1, on=nc.vector)
+        for t in (0, 2, 3):
+            finish_effect(1, 0, t)
+        quantize_effect(0, 1)
+        interleave_effect(1, 0)
+        quantize_effect(1, 0)
+
+        for ts in ((0, 1), (2, 3)):
+            add_passes(1, 1, ts, NEW_PASSES)
+            add_passes(1, 1, ts, OLD_PASSES)
+            finish_effect(1, 1, ts[0])
+            finish_effect(1, 1, ts[1], on=nc.vector)
         for a in range(4):
-            score_mm(1, a, 0, [3, 4, 1, 2][a])
-        for a in range(2, 4):
-            score_out(0, a)
+            score(0, a, 0)
+            score(0, a, 1)
+            finish_score(0, a)
+        for r0 in (0, 256):
+            interleave_effect(1, 1, r0, r0 + 256, on=nc.vector)
+            quantize_effect(1, 1, r0, r0 + 256)
+        for q in range(2):
+            for a in range(4):
+                score(1, a, q)
         for a in range(4):
-            score_mm(1, a, 1)
-            score_out(1, a, on_vector=(a % 2 == 1))
+            finish_score(1, a, on=(nc.scalar, nc.vector)[a % 2])

@@ -122,23 +122,23 @@ def tile_perturb_seq_programmes_s3_kernel(
             nc.sync.dma_start(out=words_raw[i][:], in_=old_words[2 * i : 2 * i + 2].rearrange("g p b -> p g b"))
 
         nc.sync.dma_start(out=scale_cols[:], in_=pinv_old_scale.rearrange("o (n m) -> (o n) m", m=16))
-        load_new_rows(0, 0)
-        load_scale_bytes(w_scales_raw, old_scales)
         nc.sync.dma_start(out=bytes0[0][:], in_=byte_rows[:, 0:4, 0:1024])
-        load_new_rows(0, 1)
         load_y(0, 0)
         nc.sync.dma_start(out=bytes0[1][:], in_=byte_rows[:, 0:4, 1024:2048])
-        load_words(0)
         load_y(1, 0)
+        load_new_rows(0, 0)
+        load_new_rows(0, 1)
+        load_scale_bytes(w_scales_raw, old_scales)
         load_new_rows(1, 0)
         load_new_rows(1, 1)
-        load_y(0, 1)
+        load_words(0)
         load_words(1)
-        for i in range(2):
-            nc.sync.dma_start(out=bytes1[i][:], in_=byte_rows[:, 4 + 2 * i : 6 + 2 * i, :])
-        load_y(1, 1)
+        load_y(0, 1)
         load_scale_bytes(v_scales, prog_scales)
+        nc.sync.dma_start(out=bytes1[0][:], in_=byte_rows[:, 4:6, :])
+        load_y(1, 1)
         nc.sync.dma_start(out=v_words[:], in_=prog_words.rearrange("g p b -> p g b"))
+        nc.sync.dma_start(out=bytes1[1][:], in_=byte_rows[:, 6:8, :])
 
         clock_done = []
 
@@ -183,15 +183,29 @@ def tile_perturb_seq_programmes_s3_kernel(
                     src = bytes0[g // 2][:, 2 * i + a, K * (g % 2) : K * (g % 2) + K] if h == 0 else bytes1[i][:, a, K * g : K * g + K]
                     nc.vector.tensor_tensor(out=widened[h, g, i][:, a, :], in0=src.bitcast(E4M3FN), in1=scale, op=MULT)
 
+        def rows_of(h, c, i):
+            rows = new_rows[h][i][:, :, K * c : K * c + K] if c in NEW_PASSES else widened[h, c - 2, i][:]
+            return rows.bitcast(F32)
+
+        sorted_words = {}
+
+        def sort_words(c, on=nc.scalar):
+            copy = nc.scalar.copy if on is nc.scalar else nc.vector.tensor_copy
+            for i in range(2):
+                sorted_words[c, i] = tile([P, 2, K // 2], F32, "sorted%d_%d" % (c, i), "sorted%d_%d" % (c % 2, i))
+                copy(
+                    out=sorted_words[c, i][:].rearrange("p a (u w) -> p a u w", u=2),
+                    in_=rows_of(1, c, i).rearrange("p a (w u) -> p a u w", u=2),
+                )
+
         def turn(h, c):
             for i in range(2):
                 b = take_bank(("turn", h, c, i), "turn%d_%d_%d" % (h, c, i))
                 by_word = b[:].rearrange("p (u r) -> p u r", u=2)
                 for a in range(2):
-                    rows = new_rows[h][i][:, a, K * c : K * c + K] if c in NEW_PASSES else widened[h, c - 2, i][:, a, :]
-                    pairs = rows.bitcast(F32)
                     for u in range(2):
-                        nc.tensor.transpose(by_word[:, u, P * a : P * a + P], pairs[:, u : K // 2 : 2], ident[:])
+                        words_u = rows_of(h, c, i)[:, a, u : K // 2 : 2] if h == 0 else sorted_words[c, i][:, a, P * u : P * u + P]
+                        nc.tensor.transpose(by_word[:, u, P * a : P * a + P], words_u, ident[:])
 
         grouped = {}
 
@@ -213,10 +227,10 @@ def tile_perturb_seq_programmes_s3_kernel(
         y_grouped = {}
 
         def interleave_y(q, c):
-            y_grouped[q, c] = tile([P, 4 * 512], BF16, "y_grouped%d_%d" % (q, c), "y_grouped%d" % c)
+            y_grouped[q, c] = tile([P, 4 * 512], BF16, "y_grouped%d_%d" % (q, c))
             nc.scalar.copy(
-                out=y_grouped[q, c][:].rearrange("p (t m j) -> p m t j", t=J, j=J),
-                in_=y_raw[q][c][:].rearrange("p j (m t) -> p m t j", t=J),
+                out=y_grouped[q, c][:].rearrange("p (t m j) -> p t m j", t=J, j=J),
+                in_=y_raw[q][c][:].rearrange("p j (m t) -> p t m j", t=J),
             )
 
         def quantize_y(q, c):
@@ -265,13 +279,12 @@ def tile_perturb_seq_programmes_s3_kernel(
 
         e_grouped, e_codes, e_scales = {}, {}, {}
 
-        def interleave_effect(h, q, r0=0, r1=512, on=nc.scalar):
+        def interleave_effect(h, q, r0=0, r1=512):
             if (h, q) not in e_grouped:
                 e_grouped[h, q] = tile([P, 4 * 512], BF16, "e_grouped%d_%d" % (h, q), "e_grouped%d" % q)
                 e_codes[h, q] = tile([P, 512], U32, "e_codes%d_%d" % (h, q))
                 e_scales[h, q] = tile([P, 512], U8, "e_scales%d_%d" % (h, q))
-            copy = nc.scalar.copy if on is nc.scalar else nc.vector.tensor_copy
-            copy(
+            nc.vector.tensor_copy(
                 out=e_grouped[h, q][:, J * r0 : J * r1].rearrange("p (r t) -> p r t", t=J),
                 in_=effect[h, q][:, :, r0:r1].rearrange("p t r -> p r t"),
             )
@@ -308,101 +321,117 @@ def tile_perturb_seq_programmes_s3_kernel(
 
         ALL = range(4)
 
-        keep_clock(6)
+        keep_clock(5)
         spread_scales()
-        keep_clock(4)
+        keep_clock(5)
         for g in range(4):
             widen(0, g)
-        for c in range(PASSES):
-            turn(0, c)
-            if c < PASSES - 1:
-                keep_clock(2)
-            regroup(0, c)
-            if c == 0:
-                interleave_y(0, 0)
-        turn(1, 0)
-
-        quantize_y(0, 0)
-        quantize_rows(0, 0)
+        interleave_y(0, 0)
+        turn(0, 2)
+        keep_clock(2)
+        regroup(0, 2)
         interleave_y(1, 0)
-        interleave_y(0, 1)
-        add_passes(0, 0, ALL, (0,))
+        for c in (3, 4, 1):
+            turn(0, c)
+            keep_clock(2)
+            regroup(0, c)
+        turn(0, 5)
+        keep_clock(2)
+        sort_words(0)
+        regroup(0, 5)
+        turn(0, 0)
+        regroup(0, 0)
+        turn(1, 0)
+        sort_words(1)
+
         quantize_rows(0, 2)
+        quantize_y(0, 0)
         permute_scale_bytes(0)
         permute_words(0, 0)
         add_passes(0, 0, ALL, (2,))
         quantize_rows(0, 3)
-        quantize_rows(0, 4)
-        permute_words(1, 0)
-        quantize_rows(0, 5)
-        quantize_rows(0, 1)
+        add_passes(0, 0, ALL, (3,))
         turn(1, 1)
-        regroup(1, 0)
+        interleave_y(0, 1)
+        permute_words(1, 0)
+        for c in (4, 1):
+            quantize_rows(0, c)
         regroup(1, 1)
-        add_passes(0, 0, ALL, (3, 4))
-        widen(1, 0)
+        quantize_y(1, 0)
+        quantize_rows(0, 5)
+        permute_scale_bytes(1)
+        quantize_rows(0, 0)
         quantize_y(0, 1)
         interleave_y(1, 1)
-        turn(1, 2)
-        regroup(1, 2)
-        add_passes(0, 0, ALL, (5, 1))
-        for t in ALL:
-            finish_effect(0, 0, t)
+        regroup(1, 0)
+        add_passes(0, 0, ALL, (4, 5, 0, 1))
+        for i in range(2):
+            permute_words(i, 1)
 
-        quantize_y(1, 0)
-        widen(1, 1)
+        widen(1, 0)
         quantize_y(1, 1)
-        add_passes(0, 1, (0, 1), NEW_PASSES)
-        turn(1, 3)
-        regroup(1, 3)
-        permute_scale_bytes(1)
-        permute_words(0, 1)
-        add_passes(0, 1, (2, 3), NEW_PASSES)
-        quantize_rows(1, 2)
-        permute_words(1, 1)
-        interleave_effect(0, 0)
+        widen(1, 1)
+        finish_effect(0, 0, 0)
+        finish_effect(0, 0, 1)
+        sort_words(2)
+        finish_effect(0, 0, 2)
+        finish_effect(0, 0, 3)
+        sort_words(3)
         add_passes(0, 1, (0, 1), OLD_PASSES)
         add_passes(0, 1, (2, 3), OLD_PASSES)
-        for c in (3, 0, 1):
-            quantize_rows(1, c)
-        widen(1, 2)
-        widen(1, 3)
-        finish_effect(0, 1, 0)
-        finish_effect(0, 1, 1)
-        turn(1, 4)
-        regroup(1, 4)
-        finish_effect(0, 1, 2)
-        finish_effect(0, 1, 3)
+        add_passes(0, 1, (0, 1), NEW_PASSES)
+        quantize_rows(1, 1)
+        quantize_rows(1, 0)
+        turn(1, 2)
+        turn(1, 3)
+        regroup(1, 2)
+        add_passes(0, 1, (2, 3), NEW_PASSES)
+        for t in (0, 1, 2):
+            finish_effect(0, 1, t)
+        regroup(1, 3)
 
-        add_passes(1, 0, ALL, (2, 3))
-        quantize_rows(1, 4)
-        quantize_effect(0, 0)
+        widen(1, 2)
+        quantize_rows(1, 2)
+        widen(1, 3)
+        sort_words(4)
+        finish_effect(0, 1, 3)
+        sort_words(5, on=nc.vector)
+        add_passes(1, 0, ALL, (0, 1, 2))
+        turn(1, 4)
         turn(1, 5)
+        quantize_rows(1, 3)
+        interleave_effect(0, 0)
+        regroup(1, 4)
         regroup(1, 5)
-        interleave_effect(0, 1)
+        quantize_rows(1, 4)
         quantize_rows(1, 5)
-        add_passes(1, 0, ALL, (0, 1, 4, 5))
-        finish_effect(1, 0, 1, on=nc.vector)
-        for t in (0, 2, 3):
-            finish_effect(1, 0, t)
+        quantize_effect(0, 0)
+        interleave_effect(0, 1)
         quantize_effect(0, 1)
+
+        add_passes(1, 0, ALL, (3,))
+        add_passes(1, 1, (0, 1), NEW_PASSES)
+        add_passes(1, 1, (2, 3), NEW_PASSES)
+        add_passes(1, 0, ALL, (4, 5))
+        for t in ALL:
+            finish_effect(1, 0, t)
         interleave_effect(1, 0)
         quantize_effect(1, 0)
-
         for ts in ((0, 1), (2, 3)):
-            add_passes(1, 1, ts, NEW_PASSES)
             add_passes(1, 1, ts, OLD_PASSES)
-            finish_effect(1, 1, ts[0])
-            finish_effect(1, 1, ts[1], on=nc.vector)
+        for t in (0, 1, 2):
+            finish_effect(1, 1, t)
+        finish_effect(1, 1, 3, on=nc.vector)
+
         for a in range(4):
             score(0, a, 0)
             score(0, a, 1)
             finish_score(0, a)
-        for r0 in (0, 256):
-            interleave_effect(1, 1, r0, r0 + 256, on=nc.vector)
-            quantize_effect(1, 1, r0, r0 + 256)
-        for q in range(2):
-            for a in range(4):
-                score(1, a, q)
+        for i in range(2):
+            interleave_effect(1, 1, 256 * i, 256 * i + 256)
+            quantize_effect(1, 1, 256 * i, 256 * i + 256)
+            for q in range(2):
+                for a in (2 * i, 2 * i + 1):
+                    score(1, a, q)
         for a in range(4):
             finish_score(1, a, on=(nc.scalar, nc.vector)[a % 2])

from contextlib import ExitStack

import concourse.mybir as mybir
from concourse.masks import make_identity

PERTURBATIONS, NEW, OLD, GENES, PROGRAMMES = 1024, 1024, 2048, 1024, 512
FLOPS = 2 * PERTURBATIONS * GENES * (NEW + OLD) + 2 * PERTURBATIONS * GENES * PROGRAMMES

F32 = mybir.dt.float32
BF16 = mybir.dt.bfloat16
U32 = mybir.dt.uint32
I32 = mybir.dt.int32
U8 = mybir.dt.uint8
E4M3FN = mybir.dt.float8_e4m3fn
E4M3X4 = mybir.dt.float8_e4m3fn_x4
E2M1X4 = mybir.dt.float4_e2m1fn_x4
MULT = mybir.AluOpType.mult
ADD = mybir.AluOpType.add
SUB = mybir.AluOpType.subtract
COPY = mybir.ActivationFunctionType.Copy
IDENTITY = mybir.ActivationFunctionType.Identity

P = 128
J = 4
K = P * J
NEW_PASSES = (0, 1)
OLD_PASSES = (2, 3, 4, 5)
PASSES = len(NEW_PASSES) + len(OLD_PASSES)
BANKS = 8
CLOCK_MATMULS = 20


def tile_perturb_seq_programmes_s3_kernel(
    tc,
    pinv_new,
    pinv_old_bytes,
    pinv_old_scale,
    y_new,
    old_words,
    old_scales,
    control,
    inv_sd,
    prog_words,
    prog_scales,
    precision,
    out,
):
    nc = tc.nc
    with ExitStack() as ctx:
        sbuf = ctx.enter_context(tc.tile_pool(name="sbuf", bufs=1))
        psum = ctx.enter_context(tc.psum_pool(name="psum", bufs=1))
        ctx.enter_context(tc.manual_schedule())

        def tile(shape, dtype, name, tag=None):
            return sbuf.tile(shape, dtype, name=name, tag=tag or name, align_bytes=64)

        free_banks = list(range(BANKS))
        bank_of = {}

        def take_bank(key, name):
            j = free_banks.pop(0)
            bank_of[key] = (j, psum.tile([P, 512], F32, name=name, tag="bank%d" % j))
            return bank_of[key][1]

        def last_use(key):
            free_banks.append(bank_of[key][0])
            return bank_of[key][1]

        ident = tile([P, P], F32, "ident")
        zeros = tile([P, 512], BF16, "zeros")
        scale_cols = tile([P, 16], F32, "scale_cols")
        scale_rows = tile([P, OLD], F32, "scale_rows")
        bytes0 = [tile([P, 4, 1024], U8, "bytes0_%d" % i) for i in range(2)]
        bytes1 = [tile([P, 2, OLD], U8, "bytes1_%d" % i) for i in range(2)]
        new_rows = [[tile([P, 2, NEW], BF16, "new_rows%d_%d" % (h, i)) for i in range(2)] for h in range(2)]
        y_raw = [[tile([P, J, 512], BF16, "y_raw%d_%d" % (q, c)) for c in NEW_PASSES] for q in range(2)]
        y_codes = [[tile([P, 512], U32, "y_codes%d_%d" % (q, c)) for c in NEW_PASSES] for q in range(2)]
        y_scales = [[tile([P, 512], U8, "y_scales%d_%d" % (q, c)) for c in NEW_PASSES] for q in range(2)]
        words_raw = [tile([P, 2, 2 * GENES], U8, "words_raw%d" % i) for i in range(2)]
        words = [[tile([P, 2, 1024], U8, "words%d_%d" % (q, i)) for i in range(2)] for q in range(2)]
        w_scales_raw = tile([P, 4, GENES], U8, "w_scales_raw")
        w_scales = [tile([P, 4, 512], U8, "w_scales%d" % q) for q in range(2)]
        v_words = tile([P, 2, 2 * PROGRAMMES], U8, "v_words")
        v_scales = tile([P, 2, PROGRAMMES], U8, "v_scales")
        ctl_in, isd_in, prec_in = (tile([P, 8], BF16, n) for n in ("ctl_in", "isd_in", "prec_in"))
        ctl, isd, prec = (tile([P, 8], F32, n) for n in ("ctl", "isd", "prec"))
        ctl_isd = tile([P, 8], F32, "ctl_isd")
        minus_ctl_isd = tile([P, 8], F32, "minus_ctl_isd")
        table_load = tile([P, 1], F32, "table_load")

        make_identity(nc, ident[:])
        nc.vector.memset(w_scales_raw[:].rearrange("p g n -> p (g n)").bitcast(I32), 0)
        nc.gpsimd.memset(v_scales[:].rearrange("p g n -> p (g n)").bitcast(I32), 0)
        for vec, src in ((control, ctl_in), (inv_sd, isd_in)):
            nc.gpsimd.dma_start(out=src[:].rearrange("p (q t) -> p q t", t=J), in_=vec.rearrange("(q p t) -> p q t", p=P, t=J))
        nc.gpsimd.dma_start(out=prec_in[:], in_=precision.rearrange("(p a) -> p a", a=8))
        for dst, src in ((ctl, ctl_in), (isd, isd_in), (prec, prec_in)):
            nc.gpsimd.tensor_copy(out=dst[:], in_=src[:])
        nc.gpsimd.tensor_tensor(out=ctl_isd[:], in0=ctl[:], in1=isd[:], op=MULT)
        nc.gpsimd.tensor_scalar(out=minus_ctl_isd[:], in0=ctl_isd[:], scalar1=-1.0, scalar2=0.0, op0=MULT, op1=ADD)

        nc.vector.memset(zeros[:], 0.0)
        nc.vector.memset(table_load[:], 0.0)
        nc.scalar.activation(out=table_load[:], in_=table_load[:], func=IDENTITY)

        byte_rows = pinv_old_bytes.rearrange("(p a) k -> p a k", a=8)
        cell_rows = pinv_new.rearrange("(p a) k -> p a k", a=8)

        def load_scale_bytes(dst, src):
            rows = src.rearrange("g r n -> r g n")
            for b in range(4):
                nc.sync.dma_start(out=dst[32 * b : 32 * b + 4, :, :].bitcast(I32), in_=rows[4 * b : 4 * b + 4].bitcast(I32))

        def load_new_rows(h, i):
            nc.sync.dma_start(out=new_rows[h][i][:], in_=cell_rows[:, 4 * h + 2 * i : 4 * h + 2 * i + 2, :])

        def load_y(q, c):
            src = y_new[K * c : K * c + K, 512 * q : 512 * q + 512]
            nc.sync.dma_start(out=y_raw[q][c][:], in_=src.rearrange("(p j) n -> p j n", j=J))

        def load_words(i):
            nc.sync.dma_start(out=words_raw[i][:], in_=old_words[2 * i : 2 * i + 2].rearrange("g p b -> p g b"))

        nc.sync.dma_start(out=scale_cols[:], in_=pinv_old_scale.rearrange("o (n m) -> (o n) m", m=16))
        nc.sync.dma_start(out=bytes0[0][:], in_=byte_rows[:, 0:4, 0:1024])
        load_y(0, 0)
        nc.sync.dma_start(out=bytes0[1][:], in_=byte_rows[:, 0:4, 1024:2048])
        load_y(1, 0)
        load_new_rows(0, 0)
        load_new_rows(0, 1)
        load_scale_bytes(w_scales_raw, old_scales)
        load_new_rows(1, 0)
        load_new_rows(1, 1)
        load_words(0)
        load_words(1)
        load_y(0, 1)
        load_scale_bytes(v_scales, prog_scales)
        nc.sync.dma_start(out=bytes1[0][:], in_=byte_rows[:, 4:6, :])
        load_y(1, 1)
        nc.sync.dma_start(out=v_words[:], in_=prog_words.rearrange("g p b -> p g b"))
        nc.sync.dma_start(out=bytes1[1][:], in_=byte_rows[:, 6:8, :])

        clock_done = []

        def keep_clock(n):
            for i in range(n):
                if not clock_done:
                    take_bank("clock", "clock")
                clock_done.append(i)
                nc.tensor.matmul(bank_of["clock"][1][:], lhsT=zeros[:, 0:P], rhs=zeros[:], start=True, stop=True)
            if len(clock_done) == CLOCK_MATMULS:
                last_use("clock")

        def spread_scales():
            for i in range(4):
                b = take_bank(("spread", i), "spread%d" % i)
                for m in range(4):
                    col = scale_cols[:, 4 * i + m : 4 * i + m + 1].to_broadcast([P, P])
                    nc.tensor.transpose(b[:, P * m : P * m + P], col, ident[:])
            by_cell = scale_rows[:].rearrange("p (n m) -> p n m", m=16)
            for i in range(4):
                nc.scalar.copy(out=by_cell[:, :, 4 * i : 4 * i + 4], in_=last_use(("spread", i))[:].rearrange("p (m n) -> p n m", m=4))

        def permute_words(i, q):
            nc.vector.tensor_copy(
                out=words[q][i][:].rearrange("p g (t m b) -> p g t m b", t=J, b=2),
                in_=words_raw[i][:, :, 1024 * q : 1024 * q + 1024].rearrange("p g (m t b) -> p g t m b", t=J, b=2),
            )

        def permute_scale_bytes(q):
            nc.vector.tensor_copy(
                out=w_scales[q][:].rearrange("p g (t m) -> p g t m", t=J),
                in_=w_scales_raw[:, :, 512 * q : 512 * q + 512].rearrange("p g (m t) -> p g t m", t=J),
            )

        widened = {}

        def widen(h, g):
            scale = scale_rows[:, K * g : K * g + K]
            for i in range(2):
                widened[h, g, i] = tile([P, 2, K], BF16, "widened%d_%d_%d" % (h, g, i), "widened%d_%d" % (g, i))
                for a in range(2):
                    src = bytes0[g // 2][:, 2 * i + a, K * (g % 2) : K * (g % 2) + K] if h == 0 else bytes1[i][:, a, K * g : K * g + K]
                    nc.vector.tensor_tensor(out=widened[h, g, i][:, a, :], in0=src.bitcast(E4M3FN), in1=scale, op=MULT)

        def rows_of(h, c, i):
            rows = new_rows[h][i][:, :, K * c : K * c + K] if c in NEW_PASSES else widened[h, c - 2, i][:]
            return rows.bitcast(F32)

        sorted_words = {}

        def sort_words(c, on=nc.scalar):
            copy = nc.scalar.copy if on is nc.scalar else nc.vector.tensor_copy
            for i in range(2):
                sorted_words[c, i] = tile([P, 2, K // 2], F32, "sorted%d_%d" % (c, i), "sorted%d_%d" % (c % 2, i))
                copy(
                    out=sorted_words[c, i][:].rearrange("p a (u w) -> p a u w", u=2),
                    in_=rows_of(1, c, i).rearrange("p a (w u) -> p a u w", u=2),
                )

        def turn(h, c):
            for i in range(2):
                b = take_bank(("turn", h, c, i), "turn%d_%d_%d" % (h, c, i))
                by_word = b[:].rearrange("p (u r) -> p u r", u=2)
                for a in range(2):
                    for u in range(2):
                        words_u = rows_of(h, c, i)[:, a, u : K // 2 : 2] if h == 0 else sorted_words[c, i][:, a, P * u : P * u + P]
                        nc.tensor.transpose(by_word[:, u, P * a : P * a + P], words_u, ident[:])

        grouped = {}

        def regroup(h, c):
            grouped[h, c] = tile([P, 4 * 512], BF16, "grouped%d_%d" % (h, c), "grouped%d" % c)
            for i in range(2):
                nc.scalar.copy(
                    out=grouped[h, c][:, 1024 * i : 1024 * i + 1024].bitcast(F32).rearrange("p (r u) -> p r u", u=2),
                    in_=last_use(("turn", h, c, i))[:].rearrange("p (u r) -> p r u", u=2),
                )

        codes, code_scales = {}, {}

        def quantize_rows(h, c):
            codes[h, c] = tile([P, 512], U32, "codes%d_%d" % (h, c))
            code_scales[h, c] = tile([P, 512], U8, "code_scales%d_%d" % (h, c))
            nc.vector.quantize_mx(out=codes[h, c][:].bitcast(E4M3X4), scales=code_scales[h, c][:], in_=grouped[h, c][:])

        y_grouped = {}

        def interleave_y(q, c):
            y_grouped[q, c] = tile([P, 4 * 512], BF16, "y_grouped%d_%d" % (q, c))
            nc.scalar.copy(
                out=y_grouped[q, c][:].rearrange("p (t m j) -> p t m j", t=J, j=J),
                in_=y_raw[q][c][:].rearrange("p j (m t) -> p t m j", t=J),
            )

        def quantize_y(q, c):
            nc.vector.quantize_mx(out=y_codes[q][c][:].bitcast(E4M3X4), scales=y_scales[q][c][:], in_=y_grouped[q, c][:])

        passes_added = {}

        def add_pass(h, q, t, c):
            key = (h, q, t)
            n = passes_added.get(key, 0)
            passes_added[key] = n + 1
            acc = take_bank(key, "acc%d_%d_%d" % key) if n == 0 else bank_of[key][1]
            if c in NEW_PASSES:
                cols = slice(P * t, P * t + P)
                lhs, lhs_scale = y_codes[q][c][:, cols].bitcast(E4M3X4), y_scales[q][c][:, cols]
            else:
                g = c - 2
                lhs = words[q][g // 2][:, g % 2, 2 * P * t : 2 * P * t + 2 * P].bitcast(E2M1X4)
                lhs_scale = w_scales[q][:, g, P * t : P * t + P]
            nc.tensor.matmul_mx(
                out=acc[:],
                lhsT=lhs,
                lhsT_scale=lhs_scale,
                rhs=codes[h, c][:].bitcast(E4M3X4),
                rhs_scale=code_scales[h, c][:],
                start=(n == 0),
                stop=(n == PASSES - 1),
            )

        def add_passes(h, q, ts, cs):
            for c in cs:
                for t in ts:
                    add_pass(h, q, t, c)

        effect = {}

        def finish_effect(h, q, t, on=nc.scalar):
            if (h, q) not in effect:
                effect[h, q] = tile([P, J, 512], BF16, "effect%d_%d" % (h, q), "effect%d" % q)
            acc = last_use((h, q, t))
            col = slice(4 * q + t, 4 * q + t + 1)
            if on is nc.scalar:
                nc.scalar.activation(out=effect[h, q][:, t, :], in_=acc[:], func=IDENTITY, bias=minus_ctl_isd[:, col], scale=isd[:, col])
            else:
                nc.vector.tensor_scalar(out=effect[h, q][:, t, :], in0=acc[:], scalar1=ctl[:, col], scalar2=isd[:, col], op0=SUB, op1=MULT)

        e_grouped, e_codes, e_scales = {}, {}, {}

        def interleave_effect(h, q, r0=0, r1=512):
            if (h, q) not in e_grouped:
                e_grouped[h, q] = tile([P, 4 * 512], BF16, "e_grouped%d_%d" % (h, q), "e_grouped%d" % q)
                e_codes[h, q] = tile([P, 512], U32, "e_codes%d_%d" % (h, q))
                e_scales[h, q] = tile([P, 512], U8, "e_scales%d_%d" % (h, q))
            nc.vector.tensor_copy(
                out=e_grouped[h, q][:, J * r0 : J * r1].rearrange("p (r t) -> p r t", t=J),
                in_=effect[h, q][:, :, r0:r1].rearrange("p t r -> p r t"),
            )

        def quantize_effect(h, q, r0=0, r1=512):
            nc.vector.quantize_mx(
                out=e_codes[h, q][:, r0:r1].bitcast(E4M3X4), scales=e_scales[h, q][:, r0:r1], in_=e_grouped[h, q][:, J * r0 : J * r1]
            )

        def score(h, a, q):
            b = take_bank(("score", h, a), "score%d_%d" % (h, a)) if q == 0 else bank_of["score", h, a][1]
            cols = slice(P * a, P * a + P)
            nc.tensor.matmul_mx(
                out=b[:],
                lhsT=e_codes[h, q][:, cols].bitcast(E4M3X4),
                lhsT_scale=e_scales[h, q][:, cols],
                rhs=v_words[:, q, :].bitcast(E2M1X4),
                rhs_scale=v_scales[:, q, :],
                start=(q == 0),
                stop=(q == 1),
            )

        out_rows = out.rearrange("(p a) r -> p a r", a=8)

        def finish_score(h, a, on=nc.scalar):
            b = last_use(("score", h, a))
            result = tile([P, PROGRAMMES], F32, "result%d_%d" % (h, a))
            factor = prec[:, 4 * h + a : 4 * h + a + 1]
            if on is nc.scalar:
                nc.scalar.activation(out=result[:], in_=b[:], func=COPY, scale=factor)
            else:
                nc.vector.tensor_scalar(out=result[:], in0=b[:], scalar1=factor, scalar2=None, op0=MULT)
            nc.sync.dma_start(out=out_rows[:, 4 * h + a, :], in_=result[:])

        ALL = range(4)

        keep_clock(5)
        spread_scales()
        keep_clock(5)
        for g in range(4):
            widen(0, g)
        interleave_y(0, 0)
        turn(0, 2)
        keep_clock(2)
        regroup(0, 2)
        interleave_y(1, 0)
        for c in (3, 4, 1):
            turn(0, c)
            keep_clock(2)
            regroup(0, c)
        turn(0, 5)
        keep_clock(2)
        sort_words(0)
        regroup(0, 5)
        turn(0, 0)
        regroup(0, 0)
        turn(1, 0)
        sort_words(1)

        quantize_rows(0, 2)
        quantize_y(0, 0)
        permute_scale_bytes(0)
        permute_words(0, 0)
        add_passes(0, 0, ALL, (2,))
        quantize_rows(0, 3)
        add_passes(0, 0, ALL, (3,))
        turn(1, 1)
        interleave_y(0, 1)
        permute_words(1, 0)
        for c in (4, 1):
            quantize_rows(0, c)
        regroup(1, 1)
        quantize_y(1, 0)
        quantize_rows(0, 5)
        permute_scale_bytes(1)
        quantize_rows(0, 0)
        quantize_y(0, 1)
        interleave_y(1, 1)
        regroup(1, 0)
        add_passes(0, 0, ALL, (4, 5, 0, 1))
        for i in range(2):
            permute_words(i, 1)

        widen(1, 0)
        quantize_y(1, 1)
        widen(1, 1)
        finish_effect(0, 0, 0)
        finish_effect(0, 0, 1)
        sort_words(2)
        finish_effect(0, 0, 2)
        finish_effect(0, 0, 3)
        sort_words(3)
        add_passes(0, 1, (0, 1), OLD_PASSES)
        add_passes(0, 1, (2, 3), OLD_PASSES)
        add_passes(0, 1, (0, 1), NEW_PASSES)
        quantize_rows(1, 1)
        quantize_rows(1, 0)
        turn(1, 2)
        turn(1, 3)
        regroup(1, 2)
        add_passes(0, 1, (2, 3), NEW_PASSES)
        for t in (0, 1, 2):
            finish_effect(0, 1, t)
        regroup(1, 3)

        widen(1, 2)
        quantize_rows(1, 2)
        widen(1, 3)
        sort_words(4)
        finish_effect(0, 1, 3)
        sort_words(5, on=nc.vector)
        add_passes(1, 0, ALL, (0, 1, 2))
        turn(1, 4)
        turn(1, 5)
        quantize_rows(1, 3)
        interleave_effect(0, 0)
        regroup(1, 4)
        regroup(1, 5)
        quantize_rows(1, 4)
        quantize_rows(1, 5)
        quantize_effect(0, 0)
        interleave_effect(0, 1)
        quantize_effect(0, 1)

        add_passes(1, 0, ALL, (3,))
        add_passes(1, 1, (0, 1), NEW_PASSES)
        add_passes(1, 1, (2, 3), NEW_PASSES)
        add_passes(1, 0, ALL, (4, 5))
        for t in ALL:
            finish_effect(1, 0, t)
        interleave_effect(1, 0)
        quantize_effect(1, 0)
        for ts in ((0, 1), (2, 3)):
            add_passes(1, 1, ts, OLD_PASSES)
        for t in (0, 1, 2):
            finish_effect(1, 1, t)
        finish_effect(1, 1, 3, on=nc.vector)

        for a in range(4):
            score(0, a, 0)
            score(0, a, 1)
            finish_score(0, a)
        for i in range(2):
            interleave_effect(1, 1, 256 * i, 256 * i + 256)
            quantize_effect(1, 1, 256 * i, 256 * i + 256)
            for q in range(2):
                for a in (2 * i, 2 * i + 1):
                    score(1, a, q)
        for a in range(4):
            finish_score(1, a, on=(nc.scalar, nc.vector)[a % 2])
